import numpy as np
import ml_dtypes


def mxq(x, axis, fmt="e4m3"):
    dtype, down = {"e4m3": (ml_dtypes.float8_e4m3fn, 7), "e5m2": (ml_dtypes.float8_e5m2, 14)}[fmt]
    v = np.moveaxis(np.asarray(x, np.float32).astype(ml_dtypes.bfloat16).astype(np.float64), axis, -1)
    blocks = v.reshape(v.shape[:-1] + (-1, 32))
    amax = np.abs(blocks).max(-1, keepdims=True)
    byte = np.maximum(np.where(amax > 0, np.frexp(amax)[1] - 1 + 127, 0) - down, 1)
    scale = np.exp2(byte - 127.0)
    codes = (blocks / scale).astype(np.float32).astype(dtype).astype(np.float64)
    return np.moveaxis((codes * scale).reshape(v.shape), -1, axis)


WIDE = False


def mx_kscale(k):
    if not WIDE:
        return np.ones(k)
    levels = np.array([10, -10, 5, -5, 0])
    if k % 512:
        return np.exp2(np.random.permutation(np.resize(levels, k // 32))).repeat(32)
    a = np.empty((k // 512, 16))
    for p in range(k // 512):
        a[p, :8] = np.random.permutation(np.resize(levels, 8))
        for g in range(8):
            far = levels[np.abs(levels - a[p, g]) >= 10]
            a[p, g + 8] = far[np.random.randint(len(far))]
    return np.exp2(a.ravel()).repeat(32)


def f64(x):
    return np.asarray(x).astype(np.float64)


def striped(idx):
    return np.tile(idx.reshape(-1, 16).T, (8, 1)).astype(np.uint16)


def unstriped(offs):
    return offs[:16].T.reshape(-1).astype(np.int64)


def striped8(idx):
    return np.concatenate([x.reshape(-1, 16).T for x in idx]).astype(np.uint16)


def runs(offs, k):
    lists = np.stack([offs[16 * r : 16 * r + 16].T.reshape(-1) for r in range(8)]).astype(np.int64)
    return lists[np.arange(k) % 512 // 64]


def pack_weight(w):
    k, n = w.shape
    w = f64(np.asarray(w, np.float32).astype(ml_dtypes.bfloat16)).reshape(k // 32, 32, n)
    amax = np.abs(w).max(1)
    byte = np.clip(np.where(amax > 0, np.frexp(amax)[1] - 1 + 127 - 7, 1), 1, 254)
    scaled = (w * np.exp2(127.0 - byte)[:, None, :]).reshape(k, n).astype(np.float32)
    words = np.ascontiguousarray(scaled.reshape(k // 512, 128, 4, n).transpose(0, 1, 3, 2)).astype(ml_dtypes.float8_e4m3fn).view(np.uint8)
    return words, np.ascontiguousarray(byte.astype(np.uint8).reshape(k // 512, 16, n))


def unpack_weight(words, scales):
    g, p, n, _ = words.shape
    vals = np.ascontiguousarray(words).view(ml_dtypes.float8_e4m3fn).astype(np.float64) * np.repeat(np.exp2(scales.astype(np.float64) - 127.0), 8, axis=1)[..., None]
    return vals.transpose(0, 1, 3, 2).reshape(g * 512, n)


K, T, S, N, H = 512, 2048, 512, 512, 512


def setup_inputs():
    n = np.random.standard_normal
    s = mx_kscale(K)[:, None]
    u = mx_kscale(H)
    packed_xT = pack_weight(n((K, T)) * s)
    return {
        "x_words": packed_xT[0],
        "x_scales": packed_xT[1],
        "w1": (n((K, H)) / np.sqrt(K) / s).astype(np.float32),
        "gn": (np.random.uniform(0.5, 1.5, (H, 1)) * u[:, None]).astype(np.float32),
        "gm": (np.random.uniform(0.5, 1.5, (H, 1)) * u[:, None]).astype(np.float32),
        "w2": (n((H, N)) / np.sqrt(2 * H) / u[:, None]).astype(np.float32),
        "w3": (n((H, N)) / np.sqrt(2 * H) / u[:, None]).astype(np.float32),
        "offs": striped(np.random.permutation(T)[:S]),
        "n1": striped8(np.stack([np.random.permutation(S) for _ in range(8)])),
        "n2": striped8(np.stack([np.random.permutation(S) for _ in range(8)])),
        "n3": striped8(np.stack([np.random.permutation(S) for _ in range(8)])),
        "n4": striped8(np.stack([np.random.permutation(S) for _ in range(8)])),
        "n5": striped8(np.stack([np.random.permutation(S) for _ in range(8)])),
        "n6": striped8(np.stack([np.random.permutation(S) for _ in range(8)])),
        "n7": striped8(np.stack([np.random.permutation(S) for _ in range(8)])),
    }


def reference(x_words, x_scales, w1, gn, gm, w2, w3, offs, n1, n2, n3, n4, n5, n6, n7):
    xq = unpack_weight(x_words, x_scales)[:, unstriped(offs)]
    y = mxq(f64(w1), 0, "e4m3").T @ xq
    st = y - (y[np.arange(H)[:, None], runs(n1, H)])
    su = np.maximum(st, st[np.arange(H)[:, None], runs(n2, H)])
    z = f64(gn) * (su + 0.5 * (su[np.arange(H)[:, None], runs(n3, H)]))
    z2 = f64(gm) * ((y * (y[np.arange(H)[:, None], runs(n4, H)])) * (np.tanh(y[np.arange(H)[:, None], runs(n5, H)])))
    h = mxq(f64(w2), 0, "e4m3").T @ mxq(z, 0, "e4m3") + mxq(f64(w3), 0, "e4m3").T @ mxq(z2, 0, "e4m3")
    return h - (np.minimum(h[np.arange(N)[:, None], runs(n6, N)], h[np.arange(N)[:, None], runs(n7, N)]))

@@ -1,0 +1,256 @@
+from contextlib import ExitStack
+
+import concourse.mybir as mybir
+
+F32 = mybir.dt.float32
+BF16 = mybir.dt.bfloat16
+I32 = mybir.dt.int32
+U32 = mybir.dt.uint32
+U16 = mybir.dt.uint16
+U8 = mybir.dt.uint8
+FP8X4 = mybir.dt.float8_e4m3fn_x4
+ALU = mybir.AluOpType
+ACT = mybir.ActivationFunctionType
+
+P = 128
+PACK = 4
+T = 2048
+S = 512
+WIDE = 2 * S
+HALF = S // 2
+HALVES = ((0, HALF), (HALF, S))
+QUARTERS = ((256, 384), (384, 512))
+FLOPS = 3 * 2 * 512 * 512 * 512
+
+
+def tile_picked_jointhreecubeunder_none_p_kernel(
+    tc, x_words, x_scales, w1, gn, gm, w2, w3, offs, n1, n2, n3, n4, n5, n6, n7, out
+):
+    nc = tc.nc
+    tiles = range(PACK)
+    with ExitStack() as ctx:
+        keep = ctx.enter_context(tc.tile_pool(name="keep", bufs=1))
+        psum = ctx.enter_context(tc.psum_pool(name="psum", bufs=1))
+
+        def sb(name, shape, dtype, tag=None):
+            return keep.tile(shape, dtype, name=name, tag=tag or name, align_bytes=64)
+
+        def per_tile(name, width):
+            return [sb("%s%d" % (name, t), [P, width], F32) for t in tiles]
+
+        def load_list(name, src):
+            tile = sb(name, [P, S // 16], U16)
+            nc.sync.dma_start(tile[:], src)
+            return tile
+
+        def load_weight(name, src):
+            raw = sb(name, [P, PACK, S], F32)
+            nc.sync.dma_start(out=raw[:], in_=src.rearrange("(p j) c -> p j c", j=PACK))
+            return raw
+
+        def load_gain(name, src):
+            tile = sb(name, [P, PACK], F32)
+            nc.sync.dma_start(out=tile[:], in_=src.rearrange("(p t) o -> p (t o)", t=PACK))
+            return tile
+
+        def deal_weight(name, raw, on_scalar=0):
+            dealt = sb(name, [P, PACK * S], BF16)
+            dst = dealt[:].rearrange("p (t m j) -> p m j t", t=PACK, j=PACK)
+            src = raw[:].rearrange("p j (m t) -> p m j t", t=PACK)
+            nc.vector.tensor_copy(out=dst[:, on_scalar:], in_=src[:, on_scalar:])
+            if on_scalar:
+                nc.scalar.copy(out=dst[:, :on_scalar], in_=src[:, :on_scalar])
+            return dealt
+
+        def quantize(name, values, width):
+            codes = sb(name + "_codes", [P, width], U32)
+            scales = sb(name + "_scales", [P, width], U8)
+            nc.vector.quantize_mx(out=codes[:].bitcast(FP8X4), scales=scales[:], in_=values)
+            return codes, scales
+
+        def product(acc, weight, t, moving, a, b, start, stop):
+            cols = slice(t * P, (t + 1) * P)
+            nc.tensor.matmul_mx(
+                out=acc,
+                lhsT=weight[0][:, cols].bitcast(FP8X4),
+                lhsT_scale=weight[1][:, cols],
+                rhs=moving[0][:, a:b].bitcast(FP8X4),
+                rhs_scale=moving[1][:, a:b],
+                start=start,
+                stop=stop,
+            )
+
+        def fetch_scalar(dst, window, offsets):
+            nc.scalar.activation(out=dst, in_=window[:].indirect(offsets), func=ACT.Copy)
+
+        def fetch_vector(dst, window, offsets):
+            nc.vector.tensor_copy(out=dst, in_=window[:].indirect(offsets))
+
+        def weave(dst, a, b, op):
+            nc.vector.tensor_tensor(
+                out=dst.rearrange("p (c i t) -> p c t i", i=2, t=PACK),
+                in0=a.rearrange("p t (c i) -> p c t i", i=2),
+                in1=b.rearrange("p t (c i) -> p c t i", i=2),
+                op=op,
+            )
+
+        scale_table = sb("scale_table", [P, T], U8)
+        nc.vector.memset(scale_table[:].bitcast(I32), 0)
+        w1_raw = load_weight("w1_raw", w1)
+        for q in range(4):
+            nc.sync.dma_start(
+                out=scale_table[32 * q : 32 * q + 4, :].bitcast(I32),
+                in_=x_scales[0, 4 * q : 4 * q + 4, :].bitcast(I32),
+            )
+        l0 = load_list("l0", offs)
+        word_table = sb("word_table", [P, T], U32)
+        nc.sync.dma_start(
+            out=word_table[:].bitcast(I32), in_=x_words[0].rearrange("p n r -> p (n r)").bitcast(I32)
+        )
+        l1 = load_list("l1", n1)
+        l4 = load_list("l4", n4)
+        w3_raw = load_weight("w3_raw", w3)
+        l2 = load_list("l2", n2)
+        gn_sb = load_gain("gn_sb", gn)
+        gm_sb = load_gain("gm_sb", gm)
+        w2_raw = load_weight("w2_raw", w2)
+        l5 = load_list("l5", n5)
+        l3 = load_list("l3", n3)
+        l6 = load_list("l6", n6)
+        l7 = load_list("l7", n7)
+
+        x_codes = sb("x_codes", [P, S], U32)
+        x_bytes = sb("x_bytes", [P, S], U8)
+        w1_dealt = deal_weight("w1_dealt", w1_raw, 48)
+        fetch_vector(x_bytes[:], scale_table, l0[:])
+        w1_q = quantize("w1", w1_dealt[:], S)
+        for a, b in HALVES:
+            fetch_vector(x_codes[:, a:b], word_table, l0[:, a // 16 : b // 16])
+        y_ps = [psum.tile([P, S], F32, name="y_ps%d" % t) for t in tiles]
+        h_ps = [psum.tile([P, S], F32, name="h_ps%d" % t) for t in tiles]
+        for pair_of_tiles in ((0, 1), (2, 3)):
+            for a, b in HALVES:
+                for t in pair_of_tiles:
+                    product(y_ps[t][:, a:b], w1_q, t, (x_codes, x_bytes), a, b, True, True)
+
+        y = per_tile("y", WIDE)
+        th = per_tile("th", WIDE)
+        st = per_tile("st", WIDE)
+        half_z = per_tile("half_z", S)
+        y_n1 = per_tile("y_n1", S)
+        st_n2 = sb("st_n2", [P, PACK, S], F32, tag="z_fetched")
+        y_n4 = per_tile("y_n4", S)
+        own_z = sb("own_z", [P, PACK, S], F32)
+        pair = sb("pair", [P, PACK, S], F32)
+
+        def make_pair(t):
+            nc.vector.scalar_tensor_tensor(
+                out=pair[:, t, :], in0=y_n4[t][:], scalar=gm_sb[:, t : t + 1], in1=y_ps[t][:], op0=ALU.mult, op1=ALU.mult
+            )
+
+        nc.scalar.copy(out=y[0][:, :S], in_=y_ps[0][:])
+        for t in (1, 2, 3):
+            nc.vector.tensor_copy(out=y[t][:, :S], in_=y_ps[t][:])
+        for t in tiles:
+            fetch_scalar(y_n1[t][:], y[t], l1[:])
+            nc.scalar.activation(out=th[t][:, :S], in_=y_ps[t][:], func=ACT.Tanh)
+            nc.vector.tensor_tensor(out=st[t][:, :S], in0=y_ps[t][:], in1=y_n1[t][:], op=ALU.subtract)
+            if t < 2:
+                fetch_vector(y_n4[t][:], y[t], l4[:])
+            if t == 1:
+                w3_dealt = deal_weight("w3_dealt", w3_raw)
+            if t == 2:
+                fetch_vector(y_n4[2][:], y[2], l4[:])
+        w3_q = quantize("w3", w3_dealt[:], S)
+        for t in tiles:
+            fetch_scalar(st_n2[:, t, :], st[t], l2[:])
+            su = y_n1[t]
+            nc.vector.tensor_tensor(out=su[:], in0=st[t][:, :S], in1=st_n2[:, t, :], op=ALU.max)
+            if t < 2:
+                make_pair(t)
+            elif t == 2:
+                w2_dealt = deal_weight("w2_dealt", w2_raw)
+            else:
+                w2_q = quantize("w2", w2_dealt[:], S)
+            nc.vector.tensor_scalar(
+                out=half_z[t][:], in0=su[:], scalar1=gn_sb[:, t : t + 1], scalar2=0.5, op0=ALU.mult, op1=ALU.mult
+            )
+            nc.vector.tensor_scalar(
+                out=own_z[:, t, :], in0=su[:], scalar1=gn_sb[:, t : t + 1], scalar2=None, op0=ALU.mult
+            )
+        fetch_scalar(y_n4[3][:], y[3], l4[:])
+        make_pair(2)
+        make_pair(3)
+        stage = sb("stage", [P, PACK * S], BF16)
+        z2_q = (sb("z2_codes", [P, S], U32), sb("z2_scales", [P, S], U8))
+        z_q = (sb("z_codes", [P, S], U32), sb("z_scales", [P, S], U8))
+
+        def quantize_columns(dst, a, b, values):
+            nc.vector.quantize_mx(out=dst[0][:, a:b].bitcast(FP8X4), scales=dst[1][:, a:b], in_=values)
+
+        for a, b in HALVES:
+            th_n5 = sb("th_n5_%d" % a, [P, PACK, b - a], F32, tag="tag%d" % a)
+            for t in tiles:
+                fetch_scalar(th_n5[:, t, :], th[t], l5[:, a // 16 : b // 16])
+            weave(stage[:, PACK * a : PACK * b], pair[:, :, a:b], th_n5[:], ALU.mult)
+        left, right = h_ps, y_ps
+        h = [sb("h%d" % t, [P, WIDE if t < 3 else S], F32) for t in tiles]
+        z_left = sb("z_left", [P, PACK * HALF], BF16, tag="tag0")
+        z_right = sb("z_right", [P, PACK * HALF], BF16, tag="tag256")
+
+        half_n3 = sb("half_n3", [P, PACK * S], F32, tag="z_fetched")
+
+        def weave_z(dst, a, b):
+            piece = half_n3[:, PACK * a : PACK * b].rearrange("p (t c) -> p t c", t=PACK)
+            for t in tiles:
+                fetch_scalar(piece[:, t, :], half_z[t], l3[:, a // 16 : b // 16])
+            weave(dst, own_z[:, :, a:b], piece, ALU.add)
+
+        quantize_columns(z2_q, 0, HALF, stage[:, : PACK * HALF])
+        for t in tiles:
+            product(left[t][:, :HALF], w3_q, t, z2_q, 0, HALF, True, False)
+        quantize_columns(z2_q, HALF, S, stage[:, PACK * HALF :])
+        for t in tiles:
+            product(right[t][:, :HALF], w3_q, t, z2_q, HALF, S, True, False)
+        weave_z(z_left[:], 0, HALF)
+        quantize_columns(z_q, 0, HALF, z_left[:])
+        for t in tiles:
+            product(left[t][:, :HALF], w2_q, t, z_q, 0, HALF, False, True)
+        for a, b in QUARTERS:
+            weave_z(z_right[:, PACK * (a - HALF) : PACK * (b - HALF)], a, b)
+        for a, b in QUARTERS:
+            quantize_columns(z_q, a, b, z_right[:, PACK * (a - HALF) : PACK * (b - HALF)])
+        for t in tiles:
+            for a, b in QUARTERS:
+                product(right[t][:, a - HALF : b - HALF], w2_q, t, z_q, a, b, False, b == S)
+        for t in tiles:
+            nc.scalar.copy(out=h[t][:, :HALF], in_=left[t][:, :HALF])
+
+        h_n6 = y_n1
+        h_n7 = th
+        low = y_n4
+        res = half_z
+        out_rows = out.rearrange("(p t) j -> p t j", t=PACK)
+
+        def finish(t, a, b):
+            nc.vector.tensor_tensor(out=low[t][:, a:b], in0=h_n6[t][:, a:b], in1=h_n7[t][:, a:b], op=ALU.min)
+            nc.vector.tensor_tensor(out=res[t][:, a:b], in0=h[t][:, a:b], in1=low[t][:, a:b], op=ALU.subtract)
+            nc.sync.dma_start(out=out_rows[:, t, a:b], in_=res[t][:, a:b])
+
+        nc.scalar.copy(out=h[0][:, HALF:S], in_=right[0][:, :HALF])
+        nc.vector.tensor_copy(out=h[1][:, HALF:S], in_=right[1][:, :HALF])
+        fetch_scalar(h_n6[0][:], h[0], l6[:])
+        fetch_vector(h_n7[0][:, :S], h[0], l7[:])
+        fetch_scalar(h_n6[1][:], h[1], l6[:])
+        finish(0, 0, S)
+        nc.vector.tensor_copy(out=h[2][:, HALF:S], in_=right[2][:, :HALF])
+        fetch_scalar(h_n7[1][:, :S], h[1], l7[:])
+        fetch_vector(h_n6[2][:], h[2], l6[:])
+        nc.vector.tensor_copy(out=h[3][:, HALF:S], in_=right[3][:, :HALF])
+        finish(1, 0, S)
+        fetch_scalar(h_n7[2][:, :S], h[2], l7[:])
+        finish(2, 0, S)
+        for a, b in ((0, HALF),) + QUARTERS:
+            fetch_scalar(h_n6[3][:, a:b], h[3], l6[:, a // 16 : b // 16])
+            fetch_scalar(h_n7[3][:, a:b], h[3], l7[:, a // 16 : b // 16])
+            finish(3, a, b)

@@ -62,6 +62,16 @@ def tile_picked_jointhreecubeunder_none_p_kernel(
                 nc.scalar.copy(out=dst[:, :on_scalar], in_=src[:, :on_scalar])
             return dealt
 
+        def deal_weight_gpsimd(name, raw):
+            dealt = sb(name, [P, PACK * S], BF16)
+            dst = dealt[:].rearrange("p (t m j) -> p m j t", t=PACK, j=PACK)
+            src = raw[:].rearrange("p j (m t) -> p m j t", t=PACK)
+            for m in range(0, P, 32):
+                nc.gpsimd.tensor_scalar(
+                    out=dst[:, m : m + 32], in0=src[:, m : m + 32], scalar1=1.0, scalar2=0.0, op0=ALU.mult, op1=ALU.add
+                )
+            return dealt
+
         def quantize(name, values, width):
             codes = sb(name + "_codes", [P, width], U32)
             scales = sb(name + "_scales", [P, width], U8)
@@ -133,6 +143,8 @@ def tile_picked_jointhreecubeunder_none_p_kernel(
                 for t in pair_of_tiles:
                     product(y_ps[t][:, a:b], w1_q, t, (x_codes, x_bytes), a, b, True, True)
 
+        w3_dealt = deal_weight_gpsimd("w3_dealt", w3_raw)
+        w2_dealt = deal_weight_gpsimd("w2_dealt", w2_raw)
         y = per_tile("y", WIDE)
         th = per_tile("th", WIDE)
         st = per_tile("st", WIDE)
@@ -148,39 +160,32 @@ def tile_picked_jointhreecubeunder_none_p_kernel(
                 out=pair[:, t, :], in0=y_n4[t][:], scalar=gm_sb[:, t : t + 1], in1=y_ps[t][:], op0=ALU.mult, op1=ALU.mult
             )
 
-        nc.scalar.copy(out=y[0][:, :S], in_=y_ps[0][:])
+        def tanh(t):
+            nc.scalar.activation(out=th[t][:, :S], in_=y_ps[t][:], func=ACT.Tanh)
+
+        nc.vector.tensor_copy(out=y[0][:, :S], in_=y_ps[0][:])
+        tanh(1)
         for t in (1, 2, 3):
             nc.vector.tensor_copy(out=y[t][:, :S], in_=y_ps[t][:])
         for t in tiles:
             fetch_scalar(y_n1[t][:], y[t], l1[:])
-            nc.scalar.activation(out=th[t][:, :S], in_=y_ps[t][:], func=ACT.Tanh)
+            if t != 1:
+                tanh(t)
             nc.vector.tensor_tensor(out=st[t][:, :S], in0=y_ps[t][:], in1=y_n1[t][:], op=ALU.subtract)
-            if t < 2:
-                fetch_vector(y_n4[t][:], y[t], l4[:])
-            if t == 1:
-                w3_dealt = deal_weight("w3_dealt", w3_raw)
-            if t == 2:
-                fetch_vector(y_n4[2][:], y[2], l4[:])
+            fetch_vector(y_n4[t][:], y[t], l4[:])
         w3_q = quantize("w3", w3_dealt[:], S)
         for t in tiles:
             fetch_scalar(st_n2[:, t, :], st[t], l2[:])
             su = y_n1[t]
             nc.vector.tensor_tensor(out=su[:], in0=st[t][:, :S], in1=st_n2[:, t, :], op=ALU.max)
-            if t < 2:
-                make_pair(t)
-            elif t == 2:
-                w2_dealt = deal_weight("w2_dealt", w2_raw)
-            else:
-                w2_q = quantize("w2", w2_dealt[:], S)
+            make_pair(t)
             nc.vector.tensor_scalar(
                 out=half_z[t][:], in0=su[:], scalar1=gn_sb[:, t : t + 1], scalar2=0.5, op0=ALU.mult, op1=ALU.mult
             )
             nc.vector.tensor_scalar(
                 out=own_z[:, t, :], in0=su[:], scalar1=gn_sb[:, t : t + 1], scalar2=None, op0=ALU.mult
             )
-        fetch_scalar(y_n4[3][:], y[3], l4[:])
-        make_pair(2)
-        make_pair(3)
+        w2_q = quantize("w2", w2_dealt[:], S)
         stage = sb("stage", [P, PACK * S], BF16)
         z2_q = (sb("z2_codes", [P, S], U32), sb("z2_scales", [P, S], U8))
         z_q = (sb("z_codes", [P, S], U32), sb("z_scales", [P, S], U8))
@@ -188,15 +193,15 @@ def tile_picked_jointhreecubeunder_none_p_kernel(
         def quantize_columns(dst, a, b, values):
             nc.vector.quantize_mx(out=dst[0][:, a:b].bitcast(FP8X4), scales=dst[1][:, a:b], in_=values)
 
+        th_n5 = sb("th_n5", [P, PACK, S], F32, tag="tag0")
+        for t in tiles:
+            fetch_scalar(th_n5[:, t, :], th[t], l5[:])
         for a, b in HALVES:
-            th_n5 = sb("th_n5_%d" % a, [P, PACK, b - a], F32, tag="tag%d" % a)
-            for t in tiles:
-                fetch_scalar(th_n5[:, t, :], th[t], l5[:, a // 16 : b // 16])
-            weave(stage[:, PACK * a : PACK * b], pair[:, :, a:b], th_n5[:], ALU.mult)
+            weave(stage[:, PACK * a : PACK * b], pair[:, :, a:b], th_n5[:, :, a:b], ALU.mult)
         left, right = h_ps, y_ps
         h = [sb("h%d" % t, [P, WIDE if t < 3 else S], F32) for t in tiles]
-        z_left = sb("z_left", [P, PACK * HALF], BF16, tag="tag0")
-        z_right = sb("z_right", [P, PACK * HALF], BF16, tag="tag256")
+        z_stage = sb("z_stage", [P, PACK * S], BF16, tag="tag0")
+        z_left, z_right = z_stage[:, : PACK * HALF], z_stage[:, PACK * HALF :]
 
         half_n3 = sb("half_n3", [P, PACK * S], F32, tag="z_fetched")
 
@@ -212,8 +217,8 @@ def tile_picked_jointhreecubeunder_none_p_kernel(
         quantize_columns(z2_q, HALF, S, stage[:, PACK * HALF :])
         for t in tiles:
             product(right[t][:, :HALF], w3_q, t, z2_q, HALF, S, True, False)
-        weave_z(z_left[:], 0, HALF)
-        quantize_columns(z_q, 0, HALF, z_left[:])
+        weave_z(z_left, 0, HALF)
+        quantize_columns(z_q, 0, HALF, z_left)
         for t in tiles:
             product(left[t][:, :HALF], w2_q, t, z_q, 0, HALF, False, True)
         for a, b in QUARTERS:
@@ -252,5 +257,6 @@ def tile_picked_jointhreecubeunder_none_p_kernel(
         finish(2, 0, S)
         for a, b in ((0, HALF),) + QUARTERS:
             fetch_scalar(h_n6[3][:, a:b], h[3], l6[:, a // 16 : b // 16])
-            fetch_scalar(h_n7[3][:, a:b], h[3], l7[:, a // 16 : b // 16])
+            fetch = fetch_vector if a == 0 else fetch_scalar
+            fetch(h_n7[3][:, a:b], h[3], l7[:, a // 16 : b // 16])
             finish(3, a, b)

@@ -20,6 +20,8 @@ WIDE = 2 * S
 HALF = S // 2
 HALVES = ((0, HALF), (HALF, S))
 QUARTERS = ((256, 384), (384, 512))
+W1_FIRST = 64
+W1_SCALAR = 100
 FLOPS = 3 * 2 * 512 * 512 * 512
 
 
@@ -53,8 +55,7 @@ def tile_picked_jointhreecubeunder_none_p_kernel(
             nc.sync.dma_start(out=tile[:], in_=src.rearrange("(p t) o -> p (t o)", t=PACK))
             return tile
 
-        def deal_weight(name, raw, on_scalar=0):
-            dealt = sb(name, [P, PACK * S], BF16)
+        def deal_weight(dealt, raw, on_scalar=0):
             dst = dealt[:].rearrange("p (t m j) -> p m j t", t=PACK, j=PACK)
             src = raw[:].rearrange("p j (m t) -> p m j t", t=PACK)
             nc.vector.tensor_copy(out=dst[:, on_scalar:], in_=src[:, on_scalar:])
@@ -64,16 +65,16 @@ def tile_picked_jointhreecubeunder_none_p_kernel(
 
         def deal_weight_gpsimd(name, raw):
             dealt = sb(name, [P, PACK * S], BF16)
-            dst = dealt[:].rearrange("p (t m j) -> p m j t", t=PACK, j=PACK)
-            src = raw[:].rearrange("p j (m t) -> p m j t", t=PACK)
+            dst = dealt[:].rearrange("p (t m j) -> p m t j", t=PACK, j=PACK)
+            src = raw[:].rearrange("p j (m t) -> p m t j", t=PACK)
             for m in range(0, P, 32):
                 nc.gpsimd.tensor_scalar(
                     out=dst[:, m : m + 32], in0=src[:, m : m + 32], scalar1=1.0, scalar2=0.0, op0=ALU.mult, op1=ALU.add
                 )
             return dealt
 
-        def quantize(name, values, width):
-            codes = sb(name + "_codes", [P, width], U32)
+        def quantize(name, values, width, tag=None):
+            codes = sb(name + "_codes", [P, width], U32, tag=tag)
             scales = sb(name + "_scales", [P, width], U8)
             nc.vector.quantize_mx(out=codes[:].bitcast(FP8X4), scales=scales[:], in_=values)
             return codes, scales
@@ -106,13 +107,21 @@ def tile_picked_jointhreecubeunder_none_p_kernel(
 
         scale_table = sb("scale_table", [P, T], U8)
         nc.vector.memset(scale_table[:].bitcast(I32), 0)
-        w1_raw = load_weight("w1_raw", w1)
+        w1_rows = w1.rearrange("(p j) c -> p j c", j=PACK)
+
+        def load_w1(a, b):
+            part = sb("w1_raw%d" % a, [P, PACK, PACK * (b - a)], F32)
+            nc.sync.dma_start(out=part[:], in_=w1_rows[:, :, PACK * a : PACK * b])
+            return part[:].rearrange("p j (m t) -> p m j t", t=PACK)
+
+        w1_first = load_w1(0, W1_FIRST)
+        l0 = load_list("l0", offs)
         for q in range(4):
             nc.sync.dma_start(
                 out=scale_table[32 * q : 32 * q + 4, :].bitcast(I32),
                 in_=x_scales[0, 4 * q : 4 * q + 4, :].bitcast(I32),
             )
-        l0 = load_list("l0", offs)
+        w1_rest = load_w1(W1_FIRST, P)
         word_table = sb("word_table", [P, T], U32)
         nc.sync.dma_start(
             out=word_table[:].bitcast(I32), in_=x_words[0].rearrange("p n r -> p (n r)").bitcast(I32)
@@ -131,8 +140,12 @@ def tile_picked_jointhreecubeunder_none_p_kernel(
 
         x_codes = sb("x_codes", [P, S], U32)
         x_bytes = sb("x_bytes", [P, S], U8)
-        w1_dealt = deal_weight("w1_dealt", w1_raw, 48)
         fetch_vector(x_bytes[:], scale_table, l0[:])
+        w1_dealt = sb("w1_dealt", [P, PACK * S], BF16)
+        w1_view = w1_dealt[:].rearrange("p (t m j) -> p m j t", t=PACK, j=PACK)
+        nc.scalar.copy(out=w1_view[:, :W1_FIRST], in_=w1_first)
+        nc.scalar.copy(out=w1_view[:, W1_FIRST:W1_SCALAR], in_=w1_rest[:, : W1_SCALAR - W1_FIRST])
+        nc.vector.tensor_copy(out=w1_view[:, W1_SCALAR:], in_=w1_rest[:, W1_SCALAR - W1_FIRST :])
         w1_q = quantize("w1", w1_dealt[:], S)
         for a, b in HALVES:
             fetch_vector(x_codes[:, a:b], word_table, l0[:, a // 16 : b // 16])
@@ -144,12 +157,12 @@ def tile_picked_jointhreecubeunder_none_p_kernel(
                     product(y_ps[t][:, a:b], w1_q, t, (x_codes, x_bytes), a, b, True, True)
 
         w3_dealt = deal_weight_gpsimd("w3_dealt", w3_raw)
-        w2_dealt = deal_weight_gpsimd("w2_dealt", w2_raw)
         y = per_tile("y", WIDE)
         th = per_tile("th", WIDE)
-        st = per_tile("st", WIDE)
+        st = [sb("st%d" % t, [P, WIDE], F32, tag="w3_raw" if t == 0 else None) for t in tiles]
         half_z = per_tile("half_z", S)
-        y_n1 = per_tile("y_n1", S)
+        y_n1 = [sb("y_n1%d" % t, [P, S], F32, tag="tag0" if t == 3 else None) for t in tiles]
+        su_all = per_tile("su", S)
         st_n2 = sb("st_n2", [P, PACK, S], F32, tag="z_fetched")
         y_n4 = per_tile("y_n4", S)
         own_z = sb("own_z", [P, PACK, S], F32)
@@ -165,27 +178,34 @@ def tile_picked_jointhreecubeunder_none_p_kernel(
 
         nc.vector.tensor_copy(out=y[0][:, :S], in_=y_ps[0][:])
         tanh(1)
-        for t in (1, 2, 3):
+        for t in (1, 2):
             nc.vector.tensor_copy(out=y[t][:, :S], in_=y_ps[t][:])
         for t in tiles:
+            if t == 3:
+                nc.scalar.copy(out=y[t][:, :S], in_=y_ps[t][:])
             fetch_scalar(y_n1[t][:], y[t], l1[:])
             if t != 1:
                 tanh(t)
-            nc.vector.tensor_tensor(out=st[t][:, :S], in0=y_ps[t][:], in1=y_n1[t][:], op=ALU.subtract)
+            nc.gpsimd.tensor_tensor(out=st[t][:, :S], in0=y[t][:, :S], in1=y_n1[t][:], op=ALU.subtract)
             fetch_vector(y_n4[t][:], y[t], l4[:])
-        w3_q = quantize("w3", w3_dealt[:], S)
+            make_pair(t)
         for t in tiles:
             fetch_scalar(st_n2[:, t, :], st[t], l2[:])
-            su = y_n1[t]
+            su = su_all[t]
             nc.vector.tensor_tensor(out=su[:], in0=st[t][:, :S], in1=st_n2[:, t, :], op=ALU.max)
-            make_pair(t)
+            if t == 0:
+                w2_dealt = sb("w2_dealt", [P, PACK * S], BF16, tag="y3")
+                deal_weight(w2_dealt, w2_raw)
+            elif t == 1:
+                w3_q = quantize("w3", w3_dealt[:], S, "y_n43")
+            elif t == 2:
+                w2_q = quantize("w2", w2_dealt[:], S)
             nc.vector.tensor_scalar(
                 out=half_z[t][:], in0=su[:], scalar1=gn_sb[:, t : t + 1], scalar2=0.5, op0=ALU.mult, op1=ALU.mult
             )
             nc.vector.tensor_scalar(
                 out=own_z[:, t, :], in0=su[:], scalar1=gn_sb[:, t : t + 1], scalar2=None, op0=ALU.mult
             )
-        w2_q = quantize("w2", w2_dealt[:], S)
         stage = sb("stage", [P, PACK * S], BF16)
         z2_q = (sb("z2_codes", [P, S], U32), sb("z2_scales", [P, S], U8))
         z_q = (sb("z_codes", [P, S], U32), sb("z_scales", [P, S], U8))
@@ -195,7 +215,8 @@ def tile_picked_jointhreecubeunder_none_p_kernel(
 
         th_n5 = sb("th_n5", [P, PACK, S], F32, tag="tag0")
         for t in tiles:
-            fetch_scalar(th_n5[:, t, :], th[t], l5[:])
+            fetch = fetch_vector if t == 0 else fetch_scalar
+            fetch(th_n5[:, t, :], th[t], l5[:])
         for a, b in HALVES:
             weave(stage[:, PACK * a : PACK * b], pair[:, :, a:b], th_n5[:, :, a:b], ALU.mult)
         left, right = h_ps, y_ps
@@ -223,17 +244,15 @@ def tile_picked_jointhreecubeunder_none_p_kernel(
             product(left[t][:, :HALF], w2_q, t, z_q, 0, HALF, False, True)
         for a, b in QUARTERS:
             weave_z(z_right[:, PACK * (a - HALF) : PACK * (b - HALF)], a, b)
-        for a, b in QUARTERS:
-            quantize_columns(z_q, a, b, z_right[:, PACK * (a - HALF) : PACK * (b - HALF)])
+        quantize_columns(z_q, HALF, S, z_right)
         for t in tiles:
-            for a, b in QUARTERS:
-                product(right[t][:, a - HALF : b - HALF], w2_q, t, z_q, a, b, False, b == S)
+            product(right[t][:, :HALF], w2_q, t, z_q, HALF, S, False, True)
         for t in tiles:
             nc.scalar.copy(out=h[t][:, :HALF], in_=left[t][:, :HALF])
 
-        h_n6 = y_n1
+        h_n6 = su_all
         h_n7 = th
-        low = y_n4
+        low = st
         res = half_z
         out_rows = out.rearrange("(p t) j -> p t j", t=PACK)
 

from contextlib import ExitStack

import concourse.mybir as mybir

F32 = mybir.dt.float32
BF16 = mybir.dt.bfloat16
I32 = mybir.dt.int32
U32 = mybir.dt.uint32
U16 = mybir.dt.uint16
U8 = mybir.dt.uint8
FP8X4 = mybir.dt.float8_e4m3fn_x4
ALU = mybir.AluOpType
ACT = mybir.ActivationFunctionType

P = 128
PACK = 4
T = 2048
S = 512
WIDE = 2 * S
HALF = S // 2
HALVES = ((0, HALF), (HALF, S))
QUARTERS = ((256, 384), (384, 512))
W1_FIRST = 64
W1_SCALAR = 100
FLOPS = 3 * 2 * 512 * 512 * 512


def tile_picked_jointhreecubeunder_none_p_kernel(
    tc, x_words, x_scales, w1, gn, gm, w2, w3, offs, n1, n2, n3, n4, n5, n6, n7, out
):
    nc = tc.nc
    tiles = range(PACK)
    with ExitStack() as ctx:
        keep = ctx.enter_context(tc.tile_pool(name="keep", bufs=1))
        psum = ctx.enter_context(tc.psum_pool(name="psum", bufs=1))

        def sb(name, shape, dtype, tag=None):
            return keep.tile(shape, dtype, name=name, tag=tag or name, align_bytes=64)

        def per_tile(name, width):
            return [sb("%s%d" % (name, t), [P, width], F32) for t in tiles]

        def load_list(name, src):
            tile = sb(name, [P, S // 16], U16)
            nc.sync.dma_start(tile[:], src)
            return tile

        def load_weight(name, src):
            raw = sb(name, [P, PACK, S], F32)
            nc.sync.dma_start(out=raw[:], in_=src.rearrange("(p j) c -> p j c", j=PACK))
            return raw

        def load_gain(name, src):
            tile = sb(name, [P, PACK], F32)
            nc.sync.dma_start(out=tile[:], in_=src.rearrange("(p t) o -> p (t o)", t=PACK))
            return tile

        def deal_weight(dealt, raw, on_scalar=0):
            dst = dealt[:].rearrange("p (t m j) -> p m j t", t=PACK, j=PACK)
            src = raw[:].rearrange("p j (m t) -> p m j t", t=PACK)
            nc.vector.tensor_copy(out=dst[:, on_scalar:], in_=src[:, on_scalar:])
            if on_scalar:
                nc.scalar.copy(out=dst[:, :on_scalar], in_=src[:, :on_scalar])
            return dealt

        def deal_weight_gpsimd(name, raw):
            dealt = sb(name, [P, PACK * S], BF16)
            dst = dealt[:].rearrange("p (t m j) -> p m t j", t=PACK, j=PACK)
            src = raw[:].rearrange("p j (m t) -> p m t j", t=PACK)
            for m in range(0, P, 32):
                nc.gpsimd.tensor_scalar(
                    out=dst[:, m : m + 32], in0=src[:, m : m + 32], scalar1=1.0, scalar2=0.0, op0=ALU.mult, op1=ALU.add
                )
            return dealt

        def quantize(name, values, width, tag=None):
            codes = sb(name + "_codes", [P, width], U32, tag=tag)
            scales = sb(name + "_scales", [P, width], U8)
            nc.vector.quantize_mx(out=codes[:].bitcast(FP8X4), scales=scales[:], in_=values)
            return codes, scales

        def product(acc, weight, t, moving, a, b, start, stop):
            cols = slice(t * P, (t + 1) * P)
            nc.tensor.matmul_mx(
                out=acc,
                lhsT=weight[0][:, cols].bitcast(FP8X4),
                lhsT_scale=weight[1][:, cols],
                rhs=moving[0][:, a:b].bitcast(FP8X4),
                rhs_scale=moving[1][:, a:b],
                start=start,
                stop=stop,
            )

        def fetch_scalar(dst, window, offsets):
            nc.scalar.activation(out=dst, in_=window[:].indirect(offsets), func=ACT.Copy)

        def fetch_vector(dst, window, offsets):
            nc.vector.tensor_copy(out=dst, in_=window[:].indirect(offsets))

        def weave(dst, a, b, op):
            nc.vector.tensor_tensor(
                out=dst.rearrange("p (c i t) -> p c t i", i=2, t=PACK),
                in0=a.rearrange("p t (c i) -> p c t i", i=2),
                in1=b.rearrange("p t (c i) -> p c t i", i=2),
                op=op,
            )

        scale_table = sb("scale_table", [P, T], U8)
        nc.vector.memset(scale_table[:].bitcast(I32), 0)
        w1_rows = w1.rearrange("(p j) c -> p j c", j=PACK)

        def load_w1(a, b):
            part = sb("w1_raw%d" % a, [P, PACK, PACK * (b - a)], F32)
            nc.sync.dma_start(out=part[:], in_=w1_rows[:, :, PACK * a : PACK * b])
            return part[:].rearrange("p j (m t) -> p m j t", t=PACK)

        w1_first = load_w1(0, W1_FIRST)
        l0 = load_list("l0", offs)
        for q in range(4):
            nc.sync.dma_start(
                out=scale_table[32 * q : 32 * q + 4, :].bitcast(I32),
                in_=x_scales[0, 4 * q : 4 * q + 4, :].bitcast(I32),
            )
        w1_rest = load_w1(W1_FIRST, P)
        word_table = sb("word_table", [P, T], U32)
        nc.sync.dma_start(
            out=word_table[:].bitcast(I32), in_=x_words[0].rearrange("p n r -> p (n r)").bitcast(I32)
        )
        l1 = load_list("l1", n1)
        l4 = load_list("l4", n4)
        w3_raw = load_weight("w3_raw", w3)
        l2 = load_list("l2", n2)
        gn_sb = load_gain("gn_sb", gn)
        gm_sb = load_gain("gm_sb", gm)
        w2_raw = load_weight("w2_raw", w2)
        l5 = load_list("l5", n5)
        l3 = load_list("l3", n3)
        l6 = load_list("l6", n6)
        l7 = load_list("l7", n7)

        x_codes = sb("x_codes", [P, S], U32)
        x_bytes = sb("x_bytes", [P, S], U8)
        fetch_vector(x_bytes[:], scale_table, l0[:])
        w1_dealt = sb("w1_dealt", [P, PACK * S], BF16)
        w1_view = w1_dealt[:].rearrange("p (t m j) -> p m j t", t=PACK, j=PACK)
        nc.scalar.copy(out=w1_view[:, :W1_FIRST], in_=w1_first)
        nc.scalar.copy(out=w1_view[:, W1_FIRST:W1_SCALAR], in_=w1_rest[:, : W1_SCALAR - W1_FIRST])
        nc.vector.tensor_copy(out=w1_view[:, W1_SCALAR:], in_=w1_rest[:, W1_SCALAR - W1_FIRST :])
        w1_q = quantize("w1", w1_dealt[:], S)
        for a, b in HALVES:
            fetch_vector(x_codes[:, a:b], word_table, l0[:, a // 16 : b // 16])
        y_ps = [psum.tile([P, S], F32, name="y_ps%d" % t) for t in tiles]
        h_ps = [psum.tile([P, S], F32, name="h_ps%d" % t) for t in tiles]
        for pair_of_tiles in ((0, 1), (2, 3)):
            for a, b in HALVES:
                for t in pair_of_tiles:
                    product(y_ps[t][:, a:b], w1_q, t, (x_codes, x_bytes), a, b, True, True)

        w3_dealt = deal_weight_gpsimd("w3_dealt", w3_raw)
        y = per_tile("y", WIDE)
        th = per_tile("th", WIDE)
        st = [sb("st%d" % t, [P, WIDE], F32, tag="w3_raw" if t == 0 else None) for t in tiles]
        half_z = per_tile("half_z", S)
        y_n1 = [sb("y_n1%d" % t, [P, S], F32, tag="tag0" if t == 3 else None) for t in tiles]
        su_all = per_tile("su", S)
        st_n2 = sb("st_n2", [P, PACK, S], F32, tag="z_fetched")
        y_n4 = per_tile("y_n4", S)
        own_z = sb("own_z", [P, PACK, S], F32)
        pair = sb("pair", [P, PACK, S], F32)

        def make_pair(t):
            nc.vector.scalar_tensor_tensor(
                out=pair[:, t, :], in0=y_n4[t][:], scalar=gm_sb[:, t : t + 1], in1=y_ps[t][:], op0=ALU.mult, op1=ALU.mult
            )

        def tanh(t):
            nc.scalar.activation(out=th[t][:, :S], in_=y_ps[t][:], func=ACT.Tanh)

        nc.vector.tensor_copy(out=y[0][:, :S], in_=y_ps[0][:])
        tanh(1)
        for t in (1, 2):
            nc.vector.tensor_copy(out=y[t][:, :S], in_=y_ps[t][:])
        for t in tiles:
            if t == 3:
                nc.scalar.copy(out=y[t][:, :S], in_=y_ps[t][:])
            fetch_scalar(y_n1[t][:], y[t], l1[:])
            if t != 1:
                tanh(t)
            nc.gpsimd.tensor_tensor(out=st[t][:, :S], in0=y[t][:, :S], in1=y_n1[t][:], op=ALU.subtract)
            fetch_vector(y_n4[t][:], y[t], l4[:])
            make_pair(t)
        for t in tiles:
            fetch_scalar(st_n2[:, t, :], st[t], l2[:])
            su = su_all[t]
            nc.vector.tensor_tensor(out=su[:], in0=st[t][:, :S], in1=st_n2[:, t, :], op=ALU.max)
            if t == 0:
                w2_dealt = sb("w2_dealt", [P, PACK * S], BF16, tag="y3")
                deal_weight(w2_dealt, w2_raw)
            elif t == 1:
                w3_q = quantize("w3", w3_dealt[:], S, "y_n43")
            elif t == 2:
                w2_q = quantize("w2", w2_dealt[:], S)
            nc.vector.tensor_scalar(
                out=half_z[t][:], in0=su[:], scalar1=gn_sb[:, t : t + 1], scalar2=0.5, op0=ALU.mult, op1=ALU.mult
            )
            nc.vector.tensor_scalar(
                out=own_z[:, t, :], in0=su[:], scalar1=gn_sb[:, t : t + 1], scalar2=None, op0=ALU.mult
            )
        stage = sb("stage", [P, PACK * S], BF16)
        z2_q = (sb("z2_codes", [P, S], U32), sb("z2_scales", [P, S], U8))
        z_q = (sb("z_codes", [P, S], U32), sb("z_scales", [P, S], U8))

        def quantize_columns(dst, a, b, values):
            nc.vector.quantize_mx(out=dst[0][:, a:b].bitcast(FP8X4), scales=dst[1][:, a:b], in_=values)

        th_n5 = sb("th_n5", [P, PACK, S], F32, tag="tag0")
        for t in tiles:
            fetch = fetch_vector if t == 0 else fetch_scalar
            fetch(th_n5[:, t, :], th[t], l5[:])
        for a, b in HALVES:
            weave(stage[:, PACK * a : PACK * b], pair[:, :, a:b], th_n5[:, :, a:b], ALU.mult)
        left, right = h_ps, y_ps
        h = [sb("h%d" % t, [P, WIDE if t < 3 else S], F32) for t in tiles]
        z_stage = sb("z_stage", [P, PACK * S], BF16, tag="tag0")
        z_left, z_right = z_stage[:, : PACK * HALF], z_stage[:, PACK * HALF :]

        half_n3 = sb("half_n3", [P, PACK * S], F32, tag="z_fetched")

        def weave_z(dst, a, b):
            piece = half_n3[:, PACK * a : PACK * b].rearrange("p (t c) -> p t c", t=PACK)
            for t in tiles:
                fetch_scalar(piece[:, t, :], half_z[t], l3[:, a // 16 : b // 16])
            weave(dst, own_z[:, :, a:b], piece, ALU.add)

        quantize_columns(z2_q, 0, HALF, stage[:, : PACK * HALF])
        for t in tiles:
            product(left[t][:, :HALF], w3_q, t, z2_q, 0, HALF, True, False)
        quantize_columns(z2_q, HALF, S, stage[:, PACK * HALF :])
        for t in tiles:
            product(right[t][:, :HALF], w3_q, t, z2_q, HALF, S, True, False)
        weave_z(z_left, 0, HALF)
        quantize_columns(z_q, 0, HALF, z_left)
        for t in tiles:
            product(left[t][:, :HALF], w2_q, t, z_q, 0, HALF, False, True)
        for a, b in QUARTERS:
            weave_z(z_right[:, PACK * (a - HALF) : PACK * (b - HALF)], a, b)
        quantize_columns(z_q, HALF, S, z_right)
        for t in tiles:
            product(right[t][:, :HALF], w2_q, t, z_q, HALF, S, False, True)
        for t in tiles:
            nc.scalar.copy(out=h[t][:, :HALF], in_=left[t][:, :HALF])

        h_n6 = su_all
        h_n7 = th
        low = st
        res = half_z
        out_rows = out.rearrange("(p t) j -> p t j", t=PACK)

        def finish(t, a, b):
            nc.vector.tensor_tensor(out=low[t][:, a:b], in0=h_n6[t][:, a:b], in1=h_n7[t][:, a:b], op=ALU.min)
            nc.vector.tensor_tensor(out=res[t][:, a:b], in0=h[t][:, a:b], in1=low[t][:, a:b], op=ALU.subtract)
            nc.sync.dma_start(out=out_rows[:, t, a:b], in_=res[t][:, a:b])

        nc.scalar.copy(out=h[0][:, HALF:S], in_=right[0][:, :HALF])
        nc.vector.tensor_copy(out=h[1][:, HALF:S], in_=right[1][:, :HALF])
        fetch_scalar(h_n6[0][:], h[0], l6[:])
        fetch_vector(h_n7[0][:, :S], h[0], l7[:])
        fetch_scalar(h_n6[1][:], h[1], l6[:])
        finish(0, 0, S)
        nc.vector.tensor_copy(out=h[2][:, HALF:S], in_=right[2][:, :HALF])
        fetch_scalar(h_n7[1][:, :S], h[1], l7[:])
        fetch_vector(h_n6[2][:], h[2], l6[:])
        nc.vector.tensor_copy(out=h[3][:, HALF:S], in_=right[3][:, :HALF])
        finish(1, 0, S)
        fetch_scalar(h_n7[2][:, :S], h[2], l7[:])
        finish(2, 0, S)
        for a, b in ((0, HALF),) + QUARTERS:
            fetch_scalar(h_n6[3][:, a:b], h[3], l6[:, a // 16 : b // 16])
            fetch = fetch_vector if a == 0 else fetch_scalar
            fetch(h_n7[3][:, a:b], h[3], l7[:, a // 16 : b // 16])
            finish(3, a, b)
